import numpy as np
import ml_dtypes


def mxq(x, axis, fmt="e4m3"):
    dtype, down = {"e4m3": (ml_dtypes.float8_e4m3fn, 7), "e5m2": (ml_dtypes.float8_e5m2, 14)}[fmt]
    v = np.moveaxis(np.asarray(x, np.float32).astype(ml_dtypes.bfloat16).astype(np.float64), axis, -1)
    blocks = v.reshape(v.shape[:-1] + (-1, 32))
    amax = np.abs(blocks).max(-1, keepdims=True)
    byte = np.maximum(np.where(amax > 0, np.frexp(amax)[1] - 1 + 127, 0) - down, 1)
    scale = np.exp2(byte - 127.0)
    codes = (blocks / scale).astype(np.float32).astype(dtype).astype(np.float64)
    return np.moveaxis((codes * scale).reshape(v.shape), -1, axis)


WIDE = False


def mx_kscale(k):
    if not WIDE:
        return np.ones(k)
    levels = np.array([10, -10, 5, -5, 0])
    if k % 512:
        return np.exp2(np.random.permutation(np.resize(levels, k // 32))).repeat(32)
    a = np.empty((k // 512, 16))
    for p in range(k // 512):
        a[p, :8] = np.random.permutation(np.resize(levels, 8))
        for g in range(8):
            far = levels[np.abs(levels - a[p, g]) >= 10]
            a[p, g + 8] = far[np.random.randint(len(far))]
    return np.exp2(a.ravel()).repeat(32)


def f64(x):
    return np.asarray(x).astype(np.float64)


def striped(idx):
    return np.tile(idx.reshape(-1, 16).T, (8, 1)).astype(np.uint16)


def unstriped(offs):
    return offs[:16].T.reshape(-1).astype(np.int64)


def striped8(idx):
    return np.concatenate([x.reshape(-1, 16).T for x in idx]).astype(np.uint16)


def runs(offs, k):
    lists = np.stack([offs[16 * r : 16 * r + 16].T.reshape(-1) for r in range(8)]).astype(np.int64)
    return lists[np.arange(k) % 512 // 64]


def pack_weight(w):
    k, n = w.shape
    w = f64(np.asarray(w, np.float32).astype(ml_dtypes.bfloat16)).reshape(k // 32, 32, n)
    amax = np.abs(w).max(1)
    byte = np.clip(np.where(amax > 0, np.frexp(amax)[1] - 1 + 127 - 7, 1), 1, 254)
    scaled = (w * np.exp2(127.0 - byte)[:, None, :]).reshape(k, n).astype(np.float32)
    words = np.ascontiguousarray(scaled.reshape(k // 512, 128, 4, n).transpose(0, 1, 3, 2)).astype(ml_dtypes.float8_e4m3fn).view(np.uint8)
    return words, np.ascontiguousarray(byte.astype(np.uint8).reshape(k // 512, 16, n))


def unpack_weight(words, scales):
    g, p, n, _ = words.shape
    vals = np.ascontiguousarray(words).view(ml_dtypes.float8_e4m3fn).astype(np.float64) * np.repeat(np.exp2(scales.astype(np.float64) - 127.0), 8, axis=1)[..., None]
    return vals.transpose(0, 1, 3, 2).reshape(g * 512, n)


E2M1 = np.array([0.0, 0.5, 1.0, 1.5, 2.0, 3.0, 4.0, 6.0, -0.0, -0.5, -1.0, -1.5, -2.0, -3.0, -4.0, -6.0])


def pack_fp4(w):
    k, n = w.shape
    w = f64(np.asarray(w, np.float32).astype(ml_dtypes.bfloat16)).reshape(k // 32, 32, n)
    amax = np.abs(w).max(1)
    mant, ex = np.frexp(amax / 6.0)
    byte = np.clip(np.where(amax > 0, np.where(mant > 0.5, ex, ex - 1) + 127, 1), 1, 254)
    scaled = (w * np.exp2(127.0 - byte)[:, None, :]).reshape(k, n).astype(np.float32)
    c = np.ascontiguousarray(scaled.reshape(k // 512, 128, 4, n).transpose(0, 1, 3, 2)).astype(ml_dtypes.float4_e2m1fn).view(np.uint8) & 0xF
    words = (c[..., 0::2] | (c[..., 1::2] << 4)).reshape(k // 512, 128, 2 * n)
    return np.ascontiguousarray(words), np.ascontiguousarray(byte.astype(np.uint8).reshape(k // 512, 16, n))


def unpack_fp4(words, scales):
    g, _, n = scales.shape
    words = np.ascontiguousarray(words).reshape(g, 128, n, 2)
    nib = np.empty((g, 128, n, 4), np.uint8)
    nib[..., 0::2] = words & 0xF
    nib[..., 1::2] = words >> 4
    vals = E2M1[nib] * np.repeat(np.exp2(scales.astype(np.float64) - 127.0), 8, axis=1)[..., None]
    return vals.transpose(0, 1, 3, 2).reshape(g * 512, n)


def planes(y):
    n, m = y.shape
    v = y.astype(np.float32).astype(ml_dtypes.bfloat16).astype(np.float64).reshape(n // 32, 32, m)
    top = np.abs(v).max(1)
    byte = np.clip(np.where(top > 0, np.frexp(top)[1] - 1 + 127 - 7, 1), 1, 254)
    codes = (v * np.exp2(127.0 - byte)[:, None, :]).reshape(n, m).astype(np.float32).astype(ml_dtypes.float8_e4m3fn).view(np.uint8)
    words = codes.reshape(n // 512, 128, 4, m).transpose(0, 1, 3, 2)
    return np.ascontiguousarray(words), np.ascontiguousarray(byte.astype(np.uint8).reshape(n // 512, 16, m))


K, T, S, N, G, H = 512, 2048, 512, 512, 2048, 512


def setup_inputs():
    n = np.random.standard_normal
    s = mx_kscale(K)[:, None]
    u = mx_kscale(S)
    packed_xT = pack_weight(n((K, T)) * s)
    packed_dT = pack_weight(n((K, G)) / s)
    packed_w1 = pack_fp4(n((H, N)) / np.sqrt(H) / u[:, None])
    return {
        "x_words": packed_xT[0],
        "x_scales": packed_xT[1],
        "d_words": packed_dT[0],
        "d_scales": packed_dT[1],
        "gn": (np.random.uniform(0.5, 1.5, (H, 1)) * u[:, None]).astype(np.float32),
        "w1_words": packed_w1[0],
        "w1_scales": packed_w1[1],
        "offs": striped(np.random.permutation(T)[:S]),
        "kidx": striped8(np.random.randint(0, G, (8, H))),
        "n1": striped8(np.stack([np.random.permutation(S) for _ in range(8)])),
        "n2": striped8(np.stack([np.random.permutation(S) for _ in range(8)])),
        "n3": striped8(np.stack([np.random.permutation(S) for _ in range(8)])),
    }


def reference(x_words, x_scales, d_words, d_scales, gn, w1_words, w1_scales, offs, kidx, n1, n2, n3):
    d_kidx = unpack_weight(d_words, d_scales)[np.arange(K)[:, None], runs(kidx, K)]
    xq = unpack_weight(x_words, x_scales)[:, unstriped(offs)]
    s = 0.0625 * (d_kidx.T @ xq)
    z = f64(gn) * ((np.tanh(s[np.arange(H)[:, None], runs(n1, H)] - s)) * (s[np.arange(H)[:, None], runs(n2, H)]))
    h = unpack_fp4(w1_words, w1_scales).T @ mxq(z, 0, "e4m3")
    out_0 = np.maximum(h, h[np.arange(N)[:, None], runs(n3, N)])
    return (out_0,) + planes(out_0)

@@ -1,0 +1,254 @@
+from contextlib import ExitStack
+
+import concourse.mybir as mybir
+
+F32 = mybir.dt.float32
+BF16 = mybir.dt.bfloat16
+I32 = mybir.dt.int32
+U32 = mybir.dt.uint32
+U16 = mybir.dt.uint16
+U8 = mybir.dt.uint8
+FP8X4 = mybir.dt.float8_e4m3fn_x4
+FP4X4 = mybir.dt.float4_e2m1fn_x4
+ALU = mybir.AluOpType
+ACT = mybir.ActivationFunctionType
+
+P = 128
+PACK = 4
+TABLE = 2048
+S = 512
+HALF = S // 2
+SCORE_SCALE = 0.0625
+FLOPS = 2 * 2 * 512 * 512 * 512
+
+Z_CHUNKS = ((0, 256), (256, 512))
+OUT_CHUNKS = ((0, 256), (256, 512))
+
+
+def list_cols(tile, lo, hi):
+    return tile[:, lo // 16 : hi // 16]
+
+
+def interleave(copy, dst, src):
+    copy(dst.rearrange("p (c i) t -> p c t i", i=4), src.rearrange("p t (c i) -> p c t i", i=4))
+
+
+def tile_picked_keyfdifbig_none_po_kernel(
+    tc, x_words, x_scales, d_words, d_scales, gn, w1_words, w1_scales, offs, kidx, n1, n2, n3, out_0, out_1, out_2
+):
+    nc = tc.nc
+    with ExitStack() as ctx:
+        keep = ctx.enter_context(tc.tile_pool(name="keep", bufs=1))
+        psum = ctx.enter_context(tc.psum_pool(name="psum", bufs=1))
+
+        def tile(name, shape, dtype):
+            return keep.tile(shape, dtype, name=name, align_bytes=64)
+
+        kidx_sb = tile("kidx_sb", [P, S // 16], U16)
+        offs_sb = tile("offs_sb", [P, S // 16], U16)
+        n1_sb = tile("n1_sb", [P, S // 16], U16)
+        n2_sb = tile("n2_sb", [P, S // 16], U16)
+        n3_sb = tile("n3_sb", [P, S // 16], U16)
+        d_table = tile("d_table", [P, TABLE], U32)
+        x_table = tile("x_table", [P, TABLE], U32)
+        ds_table = tile("ds_table", [P, TABLE], U8)
+        xs_table = tile("xs_table", [P, TABLE], U8)
+        w_raw = tile("w_raw", [P, 2 * S], U8)
+        ws_raw = tile("ws_raw", [P, S], U8)
+        gain_raw = tile("gain_raw", [P, PACK], F32)
+        gain = tile("gain", [P, PACK], F32)
+        warm_in = tile("warm_in", [P, 1], F32)
+        warm_out = tile("warm_out", [P, 1], F32)
+
+        nc.sync.dma_start(kidx_sb[:], kidx)
+        ds_rows = d_scales[0].bitcast(I32)
+        nc.sync.dma_start(ds_table[:].bitcast(I32), ds_rows.unsqueeze(1).broadcast_to([16, 8, TABLE // 4]))
+        nc.sync.dma_start(offs_sb[:], offs)
+        xs_rows = x_scales[0].bitcast(I32)
+        for q in range(4):
+            nc.sync.dma_start(
+                xs_table[:].bitcast(I32)[32 * q : 32 * q + 32, :],
+                xs_rows[4 * q : 4 * q + 4, :].unsqueeze(0).broadcast_to([8, 4, TABLE // 4]),
+            )
+        nc.sync.dma_start(d_table[:].bitcast(I32), d_words[0].rearrange("p n t -> p (n t)").bitcast(I32))
+        nc.sync.dma_start(x_table[:].bitcast(I32), x_words[0].rearrange("p n t -> p (n t)").bitcast(I32))
+        nc.sync.dma_start(n1_sb[:], n1)
+        nc.sync.dma_start(n2_sb[:], n2)
+        nc.sync.dma_start(n3_sb[:], n3)
+        nc.vector.memset(warm_in[:], 0.0)
+        nc.scalar.activation(warm_out[:], warm_in[:], ACT.Tanh)
+        nc.gpsimd.memset(ws_raw[:].bitcast(I32), 0)
+        nc.gpsimd.dma_start(w_raw[:].bitcast(I32), w1_words[0].bitcast(I32))
+        ws_rows = w1_scales[0].bitcast(I32)
+        for q in range(4):
+            nc.gpsimd.dma_start(ws_raw[:].bitcast(I32)[32 * q : 32 * q + 4, :], ws_rows[4 * q : 4 * q + 4, :])
+        nc.gpsimd.dma_start(gain_raw[:], gn.rearrange("(p t) o -> p (t o)", t=PACK))
+
+        ds_picked = tile("ds_picked", [P, S], U8)
+        ds_dealt = tile("ds_dealt", [P, S], U8)
+        d_picked = tile("d_picked", [P, S], U32)
+        d_dealt = tile("d_dealt", [P, S], U32)
+        xs_picked = tile("xs_picked", [P, S], U8)
+        x_picked = tile("x_picked", [P, S], U32)
+
+        def deal_bytes(dst, src):
+            nc.vector.tensor_copy(
+                dst[:].rearrange("p (t c i) -> p c t i", t=PACK, i=16),
+                src[:].rearrange("p (c i t) -> p c t i", t=PACK, i=16),
+            )
+
+        nc.vector.tensor_copy(ds_picked[:], ds_table[:].indirect(kidx_sb[:]))
+        deal_bytes(ds_dealt, ds_picked)
+        ds_dealt_rows = ds_dealt[:].bitcast(I32)
+        for r in range(1, 4):
+            nc.scalar.dma_start(ds_dealt_rows[r:P:32, :], ds_dealt_rows[8 * r : P : 32, :])
+        nc.vector.tensor_copy(xs_picked[:], xs_table[:].indirect(offs_sb[:]))
+        nc.vector.tensor_copy(d_picked[:], d_table[:].indirect(kidx_sb[:]))
+        nc.vector.tensor_copy(
+            d_dealt[:].bitcast(I32).rearrange("p (t c i) -> p c t i", t=PACK, i=4),
+            d_picked[:].bitcast(I32).rearrange("p (c i t) -> p c t i", t=PACK, i=4),
+        )
+        nc.vector.tensor_copy(x_picked[:], x_table[:].indirect(offs_sb[:]))
+
+        w_dealt = tile("w_dealt", [P, 2 * S], U8)
+        ws_dealt = tile("ws_dealt", [P, S], U8)
+        nc.vector.tensor_copy(
+            w_dealt[:].rearrange("p (t c i e) -> p c t i e", t=PACK, i=8, e=2),
+            w_raw[:].rearrange("p (c i t e) -> p c t i e", t=PACK, i=8, e=2),
+        )
+        deal_bytes(ws_dealt, ws_raw)
+        nc.scalar.activation(gain[:], gain_raw[:], ACT.Copy, scale=SCORE_SCALE)
+
+        s_banks = [psum.tile([P, S], F32, name="s_bank%d" % t) for t in range(PACK)]
+        h_banks = [psum.tile([P, S], F32, name="h_bank%d" % t) for t in range(PACK)]
+        for t in range(PACK):
+            cols = slice(t * P, (t + 1) * P)
+            nc.tensor.matmul_mx(
+                s_banks[t][:],
+                lhsT=d_dealt[:, cols].bitcast(FP8X4),
+                lhsT_scale=ds_dealt[:, cols],
+                rhs=x_picked[:].bitcast(FP8X4),
+                rhs_scale=xs_picked[:],
+                start=True,
+                stop=True,
+            )
+
+        s_window = [tile("s_window%d" % t, [P, S], F32) for t in range(PACK)]
+        s_plain = [tile("s_plain%d" % t, [P, S], F32) for t in range(PACK)]
+        s_gained = [tile("s_gained%d" % t, [P, S], F32) for t in range(PACK)]
+        diff = [tile("diff%d" % t, [P, S], F32) for t in range(PACK)]
+        tanh = [tile("tanh%d" % t, [P, S], F32) for t in range(PACK)]
+        z = [tile("z%d" % lo, [P, PACK, hi - lo], F32) for lo, hi in Z_CHUNKS]
+
+        def scores_out(t):
+            nc.scalar.activation(s_window[t][:], s_banks[t][:], ACT.Copy, scale=SCORE_SCALE)
+            nc.scalar.activation(s_plain[t][:], s_banks[t][:], ACT.Copy, scale=SCORE_SCALE)
+
+        def difference(t):
+            for lo in (0, HALF):
+                nc.vector.tensor_tensor(
+                    diff[t][:, lo : lo + HALF],
+                    s_window[t][:].indirect(list_cols(n1_sb, lo, lo + HALF)),
+                    s_plain[t][:, lo : lo + HALF],
+                    ALU.subtract,
+                )
+
+        def squash(t):
+            nc.scalar.activation(tanh[t][:], diff[t][:], ACT.Tanh)
+            nc.scalar.activation(s_gained[t][:], s_banks[t][:], ACT.Copy, scale=gain[:, t : t + 1])
+
+        def product(t, c):
+            lo, hi = Z_CHUNKS[c]
+            nc.vector.tensor_tensor(
+                z[c][:, t, :], s_gained[t][:].indirect(list_cols(n2_sb, lo, hi)), tanh[t][:, lo:hi], ALU.mult
+            )
+
+        chunks = range(len(Z_CHUNKS))
+        scores_out(0)
+        scores_out(1)
+        difference(0)
+        difference(1)
+        squash(0)
+        scores_out(2)
+        for c in chunks:
+            product(0, c)
+        difference(2)
+        squash(1)
+        scores_out(3)
+        for c in chunks:
+            product(1, c)
+        difference(3)
+        squash(2)
+        squash(3)
+
+        h_window = [tile("h_window%d" % t, [P, S], F32) for t in range(PACK)]
+        z_codes = tile("z_codes", [P, S], U32)
+        z_scales = tile("z_scales", [P, S], U8)
+        z_bf = [tile("z_bf%d" % lo, [P, hi - lo, PACK], BF16) for lo, hi in Z_CHUNKS]
+
+        def second_product(c):
+            lo, hi = Z_CHUNKS[c]
+            nc.vector.quantize_mx(
+                z_codes[:, lo:hi].bitcast(FP8X4), z_scales[:, lo:hi], z_bf[c][:].rearrange("p j t -> p (j t)")
+            )
+            for t in range(PACK):
+                nc.tensor.matmul_mx(
+                    h_banks[t][:, lo:hi],
+                    lhsT=w_dealt[:, 2 * P * t : 2 * P * (t + 1)].bitcast(FP4X4),
+                    lhsT_scale=ws_dealt[:, P * t : P * (t + 1)],
+                    rhs=z_codes[:, lo:hi].bitcast(FP8X4),
+                    rhs_scale=z_scales[:, lo:hi],
+                    start=True,
+                    stop=True,
+                )
+            for t in range(PACK):
+                nc.scalar.copy(h_window[t][:, lo:hi], h_banks[t][:, lo:hi])
+
+        last = len(Z_CHUNKS) - 1
+        for c in chunks:
+            product(2, c)
+            product(3, c)
+            interleave(nc.vector.tensor_copy if c == last else nc.scalar.copy, z_bf[c][:], z[c][:])
+            if c > 0:
+                second_product(c - 1)
+        second_product(last)
+
+        out_codes = tile("out_codes", [P, S], U32)
+        out_scales = tile("out_scales", [P, S], U8)
+        out_rows = out_0.rearrange("(p t) j -> p t j", t=PACK)
+        word_rows = out_1[0].rearrange("p j t -> p (j t)").bitcast(I32)
+        fetched = [tile("fetched%d" % lo, [P, PACK, hi - lo], F32) for lo, hi in OUT_CHUNKS]
+        result = [tile("result%d" % lo, [P, PACK, hi - lo], F32) for lo, hi in OUT_CHUNKS]
+        result_bf = [tile("result_bf%d" % lo, [P, hi - lo, PACK], BF16) for lo, hi in OUT_CHUNKS]
+
+        def fetch(c, t):
+            lo, hi = OUT_CHUNKS[c]
+            nc.vector.tensor_copy(fetched[c][:, t, :], h_window[t][:].indirect(list_cols(n3_sb, lo, hi)))
+
+        def larger(c, t):
+            lo, hi = OUT_CHUNKS[c]
+            nc.vector.tensor_tensor(result[c][:, t, :], fetched[c][:, t, :], h_window[t][:, lo:hi], ALU.max)
+            nc.sync.dma_start(out_rows[:, t, lo:hi], result[c][:, t, :])
+
+        def planes(c):
+            lo, hi = OUT_CHUNKS[c]
+            nc.vector.quantize_mx(
+                out_codes[:, lo:hi].bitcast(FP8X4), out_scales[:, lo:hi], result_bf[c][:].rearrange("p j t -> p (j t)")
+            )
+            nc.sync.dma_start(word_rows[:, lo:hi], out_codes[:].bitcast(I32)[:, lo:hi])
+
+        steps = [(c, t) for c in range(len(OUT_CHUNKS)) for t in range(PACK)]
+        last = len(OUT_CHUNKS) - 1
+        fetch(*steps[0])
+        for n, (c, t) in enumerate(steps):
+            if n + 1 < len(steps):
+                fetch(*steps[n + 1])
+            larger(c, t)
+            if t == PACK - 1:
+                interleave(nc.vector.tensor_copy if c == last else nc.scalar.copy, result_bf[c][:], result[c][:])
+                if c > 0:
+                    planes(c - 1)
+        planes(last)
+        scale_rows = out_2[0].bitcast(I32)
+        for q in range(4):
+            nc.scalar.dma_start(scale_rows[4 * q : 4 * q + 4, :], out_scales[:].bitcast(I32)[32 * q : 32 * q + 4, :])

@@ -22,7 +22,7 @@ SCORE_SCALE = 0.0625
 FLOPS = 2 * 2 * 512 * 512 * 512
 
 Z_CHUNKS = ((0, 256), (256, 512))
-OUT_CHUNKS = ((0, 256), (256, 512))
+OUT_CHUNKS = ((0, 384), (384, 512))
 
 
 def list_cols(tile, lo, hi):
@@ -39,6 +39,7 @@ def tile_picked_keyfdifbig_none_po_kernel(
     nc = tc.nc
     with ExitStack() as ctx:
         keep = ctx.enter_context(tc.tile_pool(name="keep", bufs=1))
+        reuse = ctx.enter_context(tc.tile_pool(name="reuse", bufs=1))
         psum = ctx.enter_context(tc.psum_pool(name="psum", bufs=1))
 
         def tile(name, shape, dtype):
@@ -49,8 +50,8 @@ def tile_picked_keyfdifbig_none_po_kernel(
         n1_sb = tile("n1_sb", [P, S // 16], U16)
         n2_sb = tile("n2_sb", [P, S // 16], U16)
         n3_sb = tile("n3_sb", [P, S // 16], U16)
-        d_table = tile("d_table", [P, TABLE], U32)
-        x_table = tile("x_table", [P, TABLE], U32)
+        d_table = reuse.tile([P, TABLE], U32, name="d_table", offset=4 * TABLE, align_bytes=64)
+        x_table = reuse.tile([P, TABLE], U32, name="x_table", offset=0, align_bytes=64)
         ds_table = tile("ds_table", [P, TABLE], U8)
         xs_table = tile("xs_table", [P, TABLE], U8)
         w_raw = tile("w_raw", [P, 2 * S], U8)
@@ -60,29 +61,25 @@ def tile_picked_keyfdifbig_none_po_kernel(
         warm_in = tile("warm_in", [P, 1], F32)
         warm_out = tile("warm_out", [P, 1], F32)
 
+        nc.gpsimd.memset(ds_table[:].bitcast(I32), 0)
+        nc.vector.memset(xs_table[:].bitcast(I32), 0)
+        nc.vector.memset(warm_in[:], 0.0)
+
         nc.sync.dma_start(kidx_sb[:], kidx)
-        ds_rows = d_scales[0].bitcast(I32)
-        nc.sync.dma_start(ds_table[:].bitcast(I32), ds_rows.unsqueeze(1).broadcast_to([16, 8, TABLE // 4]))
-        nc.sync.dma_start(offs_sb[:], offs)
+        nc.sync.dma_start(ds_table[:].bitcast(I32)[0:P:8, :], d_scales[0].bitcast(I32))
         xs_rows = x_scales[0].bitcast(I32)
         for q in range(4):
-            nc.sync.dma_start(
-                xs_table[:].bitcast(I32)[32 * q : 32 * q + 32, :],
-                xs_rows[4 * q : 4 * q + 4, :].unsqueeze(0).broadcast_to([8, 4, TABLE // 4]),
-            )
+            nc.sync.dma_start(xs_table[:].bitcast(I32)[32 * q : 32 * q + 4, :], xs_rows[4 * q : 4 * q + 4, :])
+        nc.sync.dma_start(offs_sb[:], offs)
         nc.sync.dma_start(d_table[:].bitcast(I32), d_words[0].rearrange("p n t -> p (n t)").bitcast(I32))
         nc.sync.dma_start(x_table[:].bitcast(I32), x_words[0].rearrange("p n t -> p (n t)").bitcast(I32))
-        nc.sync.dma_start(n1_sb[:], n1)
-        nc.sync.dma_start(n2_sb[:], n2)
-        nc.sync.dma_start(n3_sb[:], n3)
-        nc.vector.memset(warm_in[:], 0.0)
         nc.scalar.activation(warm_out[:], warm_in[:], ACT.Tanh)
-        nc.gpsimd.memset(ws_raw[:].bitcast(I32), 0)
-        nc.gpsimd.dma_start(w_raw[:].bitcast(I32), w1_words[0].bitcast(I32))
-        ws_rows = w1_scales[0].bitcast(I32)
-        for q in range(4):
-            nc.gpsimd.dma_start(ws_raw[:].bitcast(I32)[32 * q : 32 * q + 4, :], ws_rows[4 * q : 4 * q + 4, :])
+        nc.sync.dma_start(n1_sb[:], n1)
+        nc.gpsimd.dma_start(
+            ws_raw[:].bitcast(I32), w1_scales[0].bitcast(I32).unsqueeze(1).broadcast_to([16, 8, S // 4])
+        )
         nc.gpsimd.dma_start(gain_raw[:], gn.rearrange("(p t) o -> p (t o)", t=PACK))
+        nc.gpsimd.tensor_scalar_mul(gain[:], gain_raw[:], SCORE_SCALE)
 
         ds_picked = tile("ds_picked", [P, S], U8)
         ds_dealt = tile("ds_dealt", [P, S], U8)
@@ -97,41 +94,51 @@ def tile_picked_keyfdifbig_none_po_kernel(
                 src[:].rearrange("p (c i t) -> p c t i", t=PACK, i=16),
             )
 
+        def place_scale_rows(plane):
+            rows = plane[:].bitcast(I32)
+            for r in range(1, 4):
+                nc.sync.dma_start(rows[r:P:32, :], rows[8 * r : P : 32, :])
+
         nc.vector.tensor_copy(ds_picked[:], ds_table[:].indirect(kidx_sb[:]))
         deal_bytes(ds_dealt, ds_picked)
-        ds_dealt_rows = ds_dealt[:].bitcast(I32)
-        for r in range(1, 4):
-            nc.scalar.dma_start(ds_dealt_rows[r:P:32, :], ds_dealt_rows[8 * r : P : 32, :])
+        place_scale_rows(ds_dealt)
+        nc.sync.dma_start(w_raw[:].bitcast(I32), w1_words[0].bitcast(I32))
+        nc.sync.dma_start(n2_sb[:], n2)
+        nc.sync.dma_start(n3_sb[:], n3)
         nc.vector.tensor_copy(xs_picked[:], xs_table[:].indirect(offs_sb[:]))
         nc.vector.tensor_copy(d_picked[:], d_table[:].indirect(kidx_sb[:]))
         nc.vector.tensor_copy(
             d_dealt[:].bitcast(I32).rearrange("p (t c i) -> p c t i", t=PACK, i=4),
             d_picked[:].bitcast(I32).rearrange("p (c i t) -> p c t i", t=PACK, i=4),
         )
-        nc.vector.tensor_copy(x_picked[:], x_table[:].indirect(offs_sb[:]))
-
-        w_dealt = tile("w_dealt", [P, 2 * S], U8)
-        ws_dealt = tile("ws_dealt", [P, S], U8)
+        w_dealt = reuse.tile([P, 2 * S], U8, name="w_dealt", offset=0, align_bytes=64)
+        ws_dealt = reuse.tile([P, S], U8, name="ws_dealt", offset=4 * TABLE, align_bytes=64)
+        deal_bytes(ws_dealt, ws_raw)
+        place_scale_rows(ws_dealt)
+        for lo, hi in Z_CHUNKS:
+            nc.vector.tensor_copy(x_picked[:, lo:hi], x_table[:].indirect(list_cols(offs_sb, lo, hi)))
         nc.vector.tensor_copy(
             w_dealt[:].rearrange("p (t c i e) -> p c t i e", t=PACK, i=8, e=2),
             w_raw[:].rearrange("p (c i t e) -> p c t i e", t=PACK, i=8, e=2),
         )
-        deal_bytes(ws_dealt, ws_raw)
-        nc.scalar.activation(gain[:], gain_raw[:], ACT.Copy, scale=SCORE_SCALE)
 
-        s_banks = [psum.tile([P, S], F32, name="s_bank%d" % t) for t in range(PACK)]
-        h_banks = [psum.tile([P, S], F32, name="h_bank%d" % t) for t in range(PACK)]
+        s_parts = []
         for t in range(PACK):
             cols = slice(t * P, (t + 1) * P)
-            nc.tensor.matmul_mx(
-                s_banks[t][:],
-                lhsT=d_dealt[:, cols].bitcast(FP8X4),
-                lhsT_scale=ds_dealt[:, cols],
-                rhs=x_picked[:].bitcast(FP8X4),
-                rhs_scale=xs_picked[:],
-                start=True,
-                stop=True,
-            )
+            parts = []
+            for c, (lo, hi) in enumerate(Z_CHUNKS if t == 0 else ((0, S),)):
+                bank = psum.tile([P, hi - lo], F32, name="s_bank", tag="bank%d_%d" % (t, c))
+                nc.tensor.matmul_mx(
+                    bank[:],
+                    lhsT=d_dealt[:, cols].bitcast(FP8X4),
+                    lhsT_scale=ds_dealt[:, cols],
+                    rhs=x_picked[:, lo:hi].bitcast(FP8X4),
+                    rhs_scale=xs_picked[:, lo:hi],
+                    start=True,
+                    stop=True,
+                )
+                parts.append((bank, lo, hi))
+            s_parts.append(parts)
 
         s_window = [tile("s_window%d" % t, [P, S], F32) for t in range(PACK)]
         s_plain = [tile("s_plain%d" % t, [P, S], F32) for t in range(PACK)]
@@ -141,59 +148,60 @@ def tile_picked_keyfdifbig_none_po_kernel(
         z = [tile("z%d" % lo, [P, PACK, hi - lo], F32) for lo, hi in Z_CHUNKS]
 
         def scores_out(t):
-            nc.scalar.activation(s_window[t][:], s_banks[t][:], ACT.Copy, scale=SCORE_SCALE)
-            nc.scalar.activation(s_plain[t][:], s_banks[t][:], ACT.Copy, scale=SCORE_SCALE)
+            for bank, lo, hi in s_parts[t]:
+                nc.scalar.activation(s_window[t][:, lo:hi], bank[:], ACT.Copy, scale=SCORE_SCALE)
+                nc.scalar.activation(s_plain[t][:, lo:hi], bank[:], ACT.Copy, scale=SCORE_SCALE)
+
+        def gained_out(t):
+            for bank, lo, hi in s_parts[t]:
+                nc.scalar.activation(s_gained[t][:, lo:hi], bank[:], ACT.Copy, scale=gain[:, t : t + 1])
 
         def difference(t):
-            for lo in (0, HALF):
+            for lo, hi in Z_CHUNKS:
                 nc.vector.tensor_tensor(
-                    diff[t][:, lo : lo + HALF],
-                    s_window[t][:].indirect(list_cols(n1_sb, lo, lo + HALF)),
-                    s_plain[t][:, lo : lo + HALF],
+                    diff[t][:, lo:hi],
+                    s_window[t][:].indirect(list_cols(n1_sb, lo, hi)),
+                    s_plain[t][:, lo:hi],
                     ALU.subtract,
                 )
 
-        def squash(t):
-            nc.scalar.activation(tanh[t][:], diff[t][:], ACT.Tanh)
-            nc.scalar.activation(s_gained[t][:], s_banks[t][:], ACT.Copy, scale=gain[:, t : t + 1])
-
-        def product(t, c):
+        def squash_and_multiply(t, c):
             lo, hi = Z_CHUNKS[c]
+            nc.scalar.activation(tanh[t][:, lo:hi], diff[t][:, lo:hi], ACT.Tanh)
             nc.vector.tensor_tensor(
                 z[c][:, t, :], s_gained[t][:].indirect(list_cols(n2_sb, lo, hi)), tanh[t][:, lo:hi], ALU.mult
             )
 
-        chunks = range(len(Z_CHUNKS))
-        scores_out(0)
-        scores_out(1)
-        difference(0)
-        difference(1)
-        squash(0)
-        scores_out(2)
-        for c in chunks:
-            product(0, c)
-        difference(2)
-        squash(1)
-        scores_out(3)
-        for c in chunks:
-            product(1, c)
-        difference(3)
-        squash(2)
-        squash(3)
-
-        h_window = [tile("h_window%d" % t, [P, S], F32) for t in range(PACK)]
         z_codes = tile("z_codes", [P, S], U32)
         z_scales = tile("z_scales", [P, S], U8)
         z_bf = [tile("z_bf%d" % lo, [P, hi - lo, PACK], BF16) for lo, hi in Z_CHUNKS]
 
-        def second_product(c):
-            lo, hi = Z_CHUNKS[c]
+        scores_out(0)
+        difference(0)
+        for t in range(1, PACK):
+            scores_out(t)
+            difference(t)
+            gained_out(t - 1)
+            squash_and_multiply(t - 1, 0)
+            if t == 1:
+                squash_and_multiply(0, 1)
+        gained_out(PACK - 1)
+        squash_and_multiply(PACK - 1, 0)
+        for t in range(1, PACK):
+            squash_and_multiply(t, 1)
+        interleave(nc.scalar.copy, z_bf[0][:], z[0][:])
+        interleave(nc.vector.tensor_copy, z_bf[1][:], z[1][:])
+        for c, (lo, hi) in enumerate(Z_CHUNKS):
             nc.vector.quantize_mx(
                 z_codes[:, lo:hi].bitcast(FP8X4), z_scales[:, lo:hi], z_bf[c][:].rearrange("p j t -> p (j t)")
             )
-            for t in range(PACK):
+
+        h_window = [tile("h_window%d" % t, [P, S], F32) for t in range(PACK)]
+        for t in range(PACK):
+            for c, (lo, hi) in enumerate(Z_CHUNKS):
+                h_bank = psum.tile([P, hi - lo], F32, name="h_bank", tag="bank%d_%d" % (t, c))
                 nc.tensor.matmul_mx(
-                    h_banks[t][:, lo:hi],
+                    h_bank[:],
                     lhsT=w_dealt[:, 2 * P * t : 2 * P * (t + 1)].bitcast(FP4X4),
                     lhsT_scale=ws_dealt[:, P * t : P * (t + 1)],
                     rhs=z_codes[:, lo:hi].bitcast(FP8X4),
@@ -201,17 +209,7 @@ def tile_picked_keyfdifbig_none_po_kernel(
                     start=True,
                     stop=True,
                 )
-            for t in range(PACK):
-                nc.scalar.copy(h_window[t][:, lo:hi], h_banks[t][:, lo:hi])
-
-        last = len(Z_CHUNKS) - 1
-        for c in chunks:
-            product(2, c)
-            product(3, c)
-            interleave(nc.vector.tensor_copy if c == last else nc.scalar.copy, z_bf[c][:], z[c][:])
-            if c > 0:
-                second_product(c - 1)
-        second_product(last)
+                nc.scalar.copy(h_window[t][:, lo:hi], h_bank[:])
 
         out_codes = tile("out_codes", [P, S], U32)
         out_scales = tile("out_scales", [P, S], U8)
@@ -232,9 +230,13 @@ def tile_picked_keyfdifbig_none_po_kernel(
 
         def planes(c):
             lo, hi = OUT_CHUNKS[c]
-            nc.vector.quantize_mx(
-                out_codes[:, lo:hi].bitcast(FP8X4), out_scales[:, lo:hi], result_bf[c][:].rearrange("p j t -> p (j t)")
-            )
+            for a in range(lo, hi, HALF):
+                b = min(a + HALF, hi)
+                nc.vector.quantize_mx(
+                    out_codes[:, a:b].bitcast(FP8X4),
+                    out_scales[:, a:b],
+                    result_bf[c][:, a - lo : b - lo, :].rearrange("p j t -> p (j t)"),
+                )
             nc.sync.dma_start(word_rows[:, lo:hi], out_codes[:].bitcast(I32)[:, lo:hi])
 
         steps = [(c, t) for c in range(len(OUT_CHUNKS)) for t in range(PACK)]
@@ -251,4 +253,5 @@ def tile_picked_keyfdifbig_none_po_kernel(
         planes(last)
         scale_rows = out_2[0].bitcast(I32)
         for q in range(4):
-            nc.scalar.dma_start(scale_rows[4 * q : 4 * q + 4, :], out_scales[:].bitcast(I32)[32 * q : 32 * q + 4, :])
+            queue = nc.scalar if q % 2 == 0 else nc.sync
+            queue.dma_start(scale_rows[4 * q : 4 * q + 4, :], out_scales[:].bitcast(I32)[32 * q : 32 * q + 4, :])

@@ -22,6 +22,7 @@ SCORE_SCALE = 0.0625
 FLOPS = 2 * 2 * 512 * 512 * 512
 
 Z_CHUNKS = ((0, 256), (256, 512))
+Z_VECTOR_COLS = 160
 OUT_CHUNKS = ((0, 384), (384, 512))
 
 
@@ -50,13 +51,12 @@ def tile_picked_keyfdifbig_none_po_kernel(
         n1_sb = tile("n1_sb", [P, S // 16], U16)
         n2_sb = tile("n2_sb", [P, S // 16], U16)
         n3_sb = tile("n3_sb", [P, S // 16], U16)
-        d_table = reuse.tile([P, TABLE], U32, name="d_table", offset=4 * TABLE, align_bytes=64)
+        d_table = tile("d_table", [P, TABLE], U32)
         x_table = reuse.tile([P, TABLE], U32, name="x_table", offset=0, align_bytes=64)
         ds_table = tile("ds_table", [P, TABLE], U8)
         xs_table = tile("xs_table", [P, TABLE], U8)
         w_raw = tile("w_raw", [P, 2 * S], U8)
         ws_raw = tile("ws_raw", [P, S], U8)
-        gain_raw = tile("gain_raw", [P, PACK], F32)
         gain = tile("gain", [P, PACK], F32)
         warm_in = tile("warm_in", [P, 1], F32)
         warm_out = tile("warm_out", [P, 1], F32)
@@ -66,25 +66,25 @@ def tile_picked_keyfdifbig_none_po_kernel(
         nc.vector.memset(warm_in[:], 0.0)
 
         nc.sync.dma_start(kidx_sb[:], kidx)
+        nc.sync.dma_start(offs_sb[:], offs)
         nc.sync.dma_start(ds_table[:].bitcast(I32)[0:P:8, :], d_scales[0].bitcast(I32))
+        nc.sync.dma_start(d_table[:].bitcast(I32), d_words[0].rearrange("p n t -> p (n t)").bitcast(I32))
         xs_rows = x_scales[0].bitcast(I32)
         for q in range(4):
             nc.sync.dma_start(xs_table[:].bitcast(I32)[32 * q : 32 * q + 4, :], xs_rows[4 * q : 4 * q + 4, :])
-        nc.sync.dma_start(offs_sb[:], offs)
-        nc.sync.dma_start(d_table[:].bitcast(I32), d_words[0].rearrange("p n t -> p (n t)").bitcast(I32))
         nc.sync.dma_start(x_table[:].bitcast(I32), x_words[0].rearrange("p n t -> p (n t)").bitcast(I32))
         nc.scalar.activation(warm_out[:], warm_in[:], ACT.Tanh)
         nc.sync.dma_start(n1_sb[:], n1)
         nc.gpsimd.dma_start(
             ws_raw[:].bitcast(I32), w1_scales[0].bitcast(I32).unsqueeze(1).broadcast_to([16, 8, S // 4])
         )
-        nc.gpsimd.dma_start(gain_raw[:], gn.rearrange("(p t) o -> p (t o)", t=PACK))
-        nc.gpsimd.tensor_scalar_mul(gain[:], gain_raw[:], SCORE_SCALE)
+        nc.gpsimd.dma_start(gain[:], gn.rearrange("(p t) o -> p (t o)", t=PACK))
 
         ds_picked = tile("ds_picked", [P, S], U8)
         ds_dealt = tile("ds_dealt", [P, S], U8)
         d_picked = tile("d_picked", [P, S], U32)
-        d_dealt = tile("d_dealt", [P, S], U32)
+        d_early = tile("d_early", [P, 2, P], U32)
+        d_later = reuse.tile([P, 2, P], U32, name="d_later", offset=TABLE, align_bytes=64)
         xs_picked = tile("xs_picked", [P, S], U8)
         x_picked = tile("x_picked", [P, S], U32)
 
@@ -94,33 +94,33 @@ def tile_picked_keyfdifbig_none_po_kernel(
                 src[:].rearrange("p (c i t) -> p c t i", t=PACK, i=16),
             )
 
-        def place_scale_rows(plane):
+        def place_scale_rows(queue, plane):
             rows = plane[:].bitcast(I32)
             for r in range(1, 4):
-                nc.sync.dma_start(rows[r:P:32, :], rows[8 * r : P : 32, :])
+                queue.dma_start(rows[r:P:32, :], rows[8 * r : P : 32, :])
 
         nc.vector.tensor_copy(ds_picked[:], ds_table[:].indirect(kidx_sb[:]))
         deal_bytes(ds_dealt, ds_picked)
-        place_scale_rows(ds_dealt)
+        place_scale_rows(nc.sync, ds_dealt)
         nc.sync.dma_start(w_raw[:].bitcast(I32), w1_words[0].bitcast(I32))
         nc.sync.dma_start(n2_sb[:], n2)
         nc.sync.dma_start(n3_sb[:], n3)
-        nc.vector.tensor_copy(xs_picked[:], xs_table[:].indirect(offs_sb[:]))
         nc.vector.tensor_copy(d_picked[:], d_table[:].indirect(kidx_sb[:]))
-        nc.vector.tensor_copy(
-            d_dealt[:].bitcast(I32).rearrange("p (t c i) -> p c t i", t=PACK, i=4),
-            d_picked[:].bitcast(I32).rearrange("p (c i t) -> p c t i", t=PACK, i=4),
-        )
-        w_dealt = reuse.tile([P, 2 * S], U8, name="w_dealt", offset=0, align_bytes=64)
-        ws_dealt = reuse.tile([P, S], U8, name="ws_dealt", offset=4 * TABLE, align_bytes=64)
-        deal_bytes(ws_dealt, ws_raw)
-        place_scale_rows(ws_dealt)
+        nc.vector.tensor_copy(xs_picked[:], xs_table[:].indirect(offs_sb[:]))
+        d_columns = d_picked[:].bitcast(I32).rearrange("p (c i t) -> p c t i", t=PACK, i=4)
+        nc.vector.tensor_copy(d_early[:].bitcast(I32).rearrange("p t (c i) -> p c t i", i=4), d_columns[:, :, 0:2, :])
         for lo, hi in Z_CHUNKS:
             nc.vector.tensor_copy(x_picked[:, lo:hi], x_table[:].indirect(list_cols(offs_sb, lo, hi)))
         nc.vector.tensor_copy(
-            w_dealt[:].rearrange("p (t c i e) -> p c t i e", t=PACK, i=8, e=2),
-            w_raw[:].rearrange("p (c i t e) -> p c t i e", t=PACK, i=8, e=2),
+            d_later[:].bitcast(I32).rearrange("p t (c i) -> p c t i", i=4), d_columns[:, :, 2:PACK, :]
         )
+
+        w_columns = w_raw[:].rearrange("p (m t e) -> p t m e", t=PACK, e=2)
+        ws_dealt = reuse.tile([P, S], U8, name="ws_dealt", offset=0, align_bytes=64)
+        w_first = reuse.tile([P, P, 2], U8, name="w_first", offset=S, align_bytes=64)
+        deal_bytes(ws_dealt, ws_raw)
+        place_scale_rows(nc.sync, ws_dealt)
+        nc.vector.tensor_copy(w_first[:], w_columns[:, 0, :, :])
 
         s_parts = []
         for t in range(PACK):
@@ -130,7 +130,7 @@ def tile_picked_keyfdifbig_none_po_kernel(
                 bank = psum.tile([P, hi - lo], F32, name="s_bank", tag="bank%d_%d" % (t, c))
                 nc.tensor.matmul_mx(
                     bank[:],
-                    lhsT=d_dealt[:, cols].bitcast(FP8X4),
+                    lhsT=(d_early, d_later)[t // 2][:, t % 2, :].bitcast(FP8X4),
                     lhsT_scale=ds_dealt[:, cols],
                     rhs=x_picked[:, lo:hi].bitcast(FP8X4),
                     rhs_scale=xs_picked[:, lo:hi],
@@ -150,11 +150,13 @@ def tile_picked_keyfdifbig_none_po_kernel(
         def scores_out(t):
             for bank, lo, hi in s_parts[t]:
                 nc.scalar.activation(s_window[t][:, lo:hi], bank[:], ACT.Copy, scale=SCORE_SCALE)
-                nc.scalar.activation(s_plain[t][:, lo:hi], bank[:], ACT.Copy, scale=SCORE_SCALE)
+                if t == 0:
+                    nc.vector.tensor_copy(s_plain[t][:, lo:hi], s_window[t][:, lo:hi])
+                else:
+                    nc.scalar.activation(s_plain[t][:, lo:hi], bank[:], ACT.Copy, scale=SCORE_SCALE)
 
         def gained_out(t):
-            for bank, lo, hi in s_parts[t]:
-                nc.scalar.activation(s_gained[t][:, lo:hi], bank[:], ACT.Copy, scale=gain[:, t : t + 1])
+            nc.scalar.activation(s_gained[t][:], s_window[t][:], ACT.Copy, scale=gain[:, t : t + 1])
 
         def difference(t):
             for lo, hi in Z_CHUNKS:
@@ -174,7 +176,10 @@ def tile_picked_keyfdifbig_none_po_kernel(
 
         z_codes = tile("z_codes", [P, S], U32)
         z_scales = tile("z_scales", [P, S], U8)
-        z_bf = [tile("z_bf%d" % lo, [P, hi - lo, PACK], BF16) for lo, hi in Z_CHUNKS]
+        z_bf = [
+            reuse.tile([P, HALF, PACK], BF16, name="z_bf%d" % c, offset=4 * TABLE + 2 * PACK * HALF * c, align_bytes=64)
+            for c in range(2)
+        ]
 
         scores_out(0)
         difference(0)
@@ -190,11 +195,20 @@ def tile_picked_keyfdifbig_none_po_kernel(
         for t in range(1, PACK):
             squash_and_multiply(t, 1)
         interleave(nc.scalar.copy, z_bf[0][:], z[0][:])
-        interleave(nc.vector.tensor_copy, z_bf[1][:], z[1][:])
+        interleave(nc.vector.tensor_copy, z_bf[1][:, :Z_VECTOR_COLS, :], z[1][:, :, :Z_VECTOR_COLS])
+        interleave(nc.scalar.copy, z_bf[1][:, Z_VECTOR_COLS:, :], z[1][:, :, Z_VECTOR_COLS:])
         for c, (lo, hi) in enumerate(Z_CHUNKS):
             nc.vector.quantize_mx(
                 z_codes[:, lo:hi].bitcast(FP8X4), z_scales[:, lo:hi], z_bf[c][:].rearrange("p j t -> p (j t)")
             )
+
+        w_dealt = [w_first]
+        for t in range(1, PACK):
+            w_later = reuse.tile(
+                [P, P, 2], U8, name="w_later%d" % t, offset=4 * TABLE + 2 * PACK * HALF * min(t - 1, 1) + 2 * P * t, align_bytes=64
+            )
+            nc.vector.tensor_copy(w_later[:], w_columns[:, t, :, :])
+            w_dealt.append(w_later)
 
         h_window = [tile("h_window%d" % t, [P, S], F32) for t in range(PACK)]
         for t in range(PACK):
@@ -202,7 +216,7 @@ def tile_picked_keyfdifbig_none_po_kernel(
                 h_bank = psum.tile([P, hi - lo], F32, name="h_bank", tag="bank%d_%d" % (t, c))
                 nc.tensor.matmul_mx(
                     h_bank[:],
-                    lhsT=w_dealt[:, 2 * P * t : 2 * P * (t + 1)].bitcast(FP4X4),
+                    lhsT=w_dealt[t][:].rearrange("p m e -> p (m e)").bitcast(FP4X4),
                     lhsT_scale=ws_dealt[:, P * t : P * (t + 1)],
                     rhs=z_codes[:, lo:hi].bitcast(FP8X4),
                     rhs_scale=z_scales[:, lo:hi],
@@ -246,10 +260,10 @@ def tile_picked_keyfdifbig_none_po_kernel(
             if n + 1 < len(steps):
                 fetch(*steps[n + 1])
             larger(c, t)
-            if t == PACK - 1:
-                interleave(nc.vector.tensor_copy if c == last else nc.scalar.copy, result_bf[c][:], result[c][:])
-                if c > 0:
-                    planes(c - 1)
+            if c < last and t % 2 == 1:
+                interleave(nc.scalar.copy, result_bf[c][:, :, t - 1 : t + 1], result[c][:, t - 1 : t + 1, :])
+        planes(0)
+        interleave(nc.vector.tensor_copy, result_bf[last][:], result[last][:])
         planes(last)
         scale_rows = out_2[0].bitcast(I32)
         for q in range(4):

from contextlib import ExitStack

import concourse.mybir as mybir

F32 = mybir.dt.float32
BF16 = mybir.dt.bfloat16
I32 = mybir.dt.int32
U32 = mybir.dt.uint32
U16 = mybir.dt.uint16
U8 = mybir.dt.uint8
FP8X4 = mybir.dt.float8_e4m3fn_x4
FP4X4 = mybir.dt.float4_e2m1fn_x4
ALU = mybir.AluOpType
ACT = mybir.ActivationFunctionType

P = 128
PACK = 4
TABLE = 2048
S = 512
HALF = S // 2
SCORE_SCALE = 0.0625
FLOPS = 2 * 2 * 512 * 512 * 512

Z_CHUNKS = ((0, 256), (256, 512))
Z_VECTOR_COLS = 160
OUT_CHUNKS = ((0, 384), (384, 512))


def list_cols(tile, lo, hi):
    return tile[:, lo // 16 : hi // 16]


def interleave(copy, dst, src):
    copy(dst.rearrange("p (c i) t -> p c t i", i=4), src.rearrange("p t (c i) -> p c t i", i=4))


def tile_picked_keyfdifbig_none_po_kernel(
    tc, x_words, x_scales, d_words, d_scales, gn, w1_words, w1_scales, offs, kidx, n1, n2, n3, out_0, out_1, out_2
):
    nc = tc.nc
    with ExitStack() as ctx:
        keep = ctx.enter_context(tc.tile_pool(name="keep", bufs=1))
        reuse = ctx.enter_context(tc.tile_pool(name="reuse", bufs=1))
        psum = ctx.enter_context(tc.psum_pool(name="psum", bufs=1))

        def tile(name, shape, dtype):
            return keep.tile(shape, dtype, name=name, align_bytes=64)

        kidx_sb = tile("kidx_sb", [P, S // 16], U16)
        offs_sb = tile("offs_sb", [P, S // 16], U16)
        n1_sb = tile("n1_sb", [P, S // 16], U16)
        n2_sb = tile("n2_sb", [P, S // 16], U16)
        n3_sb = tile("n3_sb", [P, S // 16], U16)
        d_table = tile("d_table", [P, TABLE], U32)
        x_table = reuse.tile([P, TABLE], U32, name="x_table", offset=0, align_bytes=64)
        ds_table = tile("ds_table", [P, TABLE], U8)
        xs_table = tile("xs_table", [P, TABLE], U8)
        w_raw = tile("w_raw", [P, 2 * S], U8)
        ws_raw = tile("ws_raw", [P, S], U8)
        gain = tile("gain", [P, PACK], F32)
        warm_in = tile("warm_in", [P, 1], F32)
        warm_out = tile("warm_out", [P, 1], F32)

        nc.gpsimd.memset(ds_table[:].bitcast(I32), 0)
        nc.vector.memset(xs_table[:].bitcast(I32), 0)
        nc.vector.memset(warm_in[:], 0.0)

        nc.sync.dma_start(kidx_sb[:], kidx)
        nc.sync.dma_start(offs_sb[:], offs)
        nc.sync.dma_start(ds_table[:].bitcast(I32)[0:P:8, :], d_scales[0].bitcast(I32))
        nc.sync.dma_start(d_table[:].bitcast(I32), d_words[0].rearrange("p n t -> p (n t)").bitcast(I32))
        xs_rows = x_scales[0].bitcast(I32)
        for q in range(4):
            nc.sync.dma_start(xs_table[:].bitcast(I32)[32 * q : 32 * q + 4, :], xs_rows[4 * q : 4 * q + 4, :])
        nc.sync.dma_start(x_table[:].bitcast(I32), x_words[0].rearrange("p n t -> p (n t)").bitcast(I32))
        nc.scalar.activation(warm_out[:], warm_in[:], ACT.Tanh)
        nc.sync.dma_start(n1_sb[:], n1)
        nc.gpsimd.dma_start(
            ws_raw[:].bitcast(I32), w1_scales[0].bitcast(I32).unsqueeze(1).broadcast_to([16, 8, S // 4])
        )
        nc.gpsimd.dma_start(gain[:], gn.rearrange("(p t) o -> p (t o)", t=PACK))

        ds_picked = tile("ds_picked", [P, S], U8)
        ds_dealt = tile("ds_dealt", [P, S], U8)
        d_picked = tile("d_picked", [P, S], U32)
        d_early = tile("d_early", [P, 2, P], U32)
        d_later = reuse.tile([P, 2, P], U32, name="d_later", offset=TABLE, align_bytes=64)
        xs_picked = tile("xs_picked", [P, S], U8)
        x_picked = tile("x_picked", [P, S], U32)

        def deal_bytes(dst, src):
            nc.vector.tensor_copy(
                dst[:].rearrange("p (t c i) -> p c t i", t=PACK, i=16),
                src[:].rearrange("p (c i t) -> p c t i", t=PACK, i=16),
            )

        def place_scale_rows(queue, plane):
            rows = plane[:].bitcast(I32)
            for r in range(1, 4):
                queue.dma_start(rows[r:P:32, :], rows[8 * r : P : 32, :])

        nc.vector.tensor_copy(ds_picked[:], ds_table[:].indirect(kidx_sb[:]))
        deal_bytes(ds_dealt, ds_picked)
        place_scale_rows(nc.sync, ds_dealt)
        nc.sync.dma_start(w_raw[:].bitcast(I32), w1_words[0].bitcast(I32))
        nc.sync.dma_start(n2_sb[:], n2)
        nc.sync.dma_start(n3_sb[:], n3)
        nc.vector.tensor_copy(d_picked[:], d_table[:].indirect(kidx_sb[:]))
        nc.vector.tensor_copy(xs_picked[:], xs_table[:].indirect(offs_sb[:]))
        d_columns = d_picked[:].bitcast(I32).rearrange("p (c i t) -> p c t i", t=PACK, i=4)
        nc.vector.tensor_copy(d_early[:].bitcast(I32).rearrange("p t (c i) -> p c t i", i=4), d_columns[:, :, 0:2, :])
        for lo, hi in Z_CHUNKS:
            nc.vector.tensor_copy(x_picked[:, lo:hi], x_table[:].indirect(list_cols(offs_sb, lo, hi)))
        nc.vector.tensor_copy(
            d_later[:].bitcast(I32).rearrange("p t (c i) -> p c t i", i=4), d_columns[:, :, 2:PACK, :]
        )

        w_columns = w_raw[:].rearrange("p (m t e) -> p t m e", t=PACK, e=2)
        ws_dealt = reuse.tile([P, S], U8, name="ws_dealt", offset=0, align_bytes=64)
        w_first = reuse.tile([P, P, 2], U8, name="w_first", offset=S, align_bytes=64)
        deal_bytes(ws_dealt, ws_raw)
        place_scale_rows(nc.sync, ws_dealt)
        nc.vector.tensor_copy(w_first[:], w_columns[:, 0, :, :])

        s_parts = []
        for t in range(PACK):
            cols = slice(t * P, (t + 1) * P)
            parts = []
            for c, (lo, hi) in enumerate(Z_CHUNKS if t == 0 else ((0, S),)):
                bank = psum.tile([P, hi - lo], F32, name="s_bank", tag="bank%d_%d" % (t, c))
                nc.tensor.matmul_mx(
                    bank[:],
                    lhsT=(d_early, d_later)[t // 2][:, t % 2, :].bitcast(FP8X4),
                    lhsT_scale=ds_dealt[:, cols],
                    rhs=x_picked[:, lo:hi].bitcast(FP8X4),
                    rhs_scale=xs_picked[:, lo:hi],
                    start=True,
                    stop=True,
                )
                parts.append((bank, lo, hi))
            s_parts.append(parts)

        s_window = [tile("s_window%d" % t, [P, S], F32) for t in range(PACK)]
        s_plain = [tile("s_plain%d" % t, [P, S], F32) for t in range(PACK)]
        s_gained = [tile("s_gained%d" % t, [P, S], F32) for t in range(PACK)]
        diff = [tile("diff%d" % t, [P, S], F32) for t in range(PACK)]
        tanh = [tile("tanh%d" % t, [P, S], F32) for t in range(PACK)]
        z = [tile("z%d" % lo, [P, PACK, hi - lo], F32) for lo, hi in Z_CHUNKS]

        def scores_out(t):
            for bank, lo, hi in s_parts[t]:
                nc.scalar.activation(s_window[t][:, lo:hi], bank[:], ACT.Copy, scale=SCORE_SCALE)
                if t == 0:
                    nc.vector.tensor_copy(s_plain[t][:, lo:hi], s_window[t][:, lo:hi])
                else:
                    nc.scalar.activation(s_plain[t][:, lo:hi], bank[:], ACT.Copy, scale=SCORE_SCALE)

        def gained_out(t):
            nc.scalar.activation(s_gained[t][:], s_window[t][:], ACT.Copy, scale=gain[:, t : t + 1])

        def difference(t):
            for lo, hi in Z_CHUNKS:
                nc.vector.tensor_tensor(
                    diff[t][:, lo:hi],
                    s_window[t][:].indirect(list_cols(n1_sb, lo, hi)),
                    s_plain[t][:, lo:hi],
                    ALU.subtract,
                )

        def squash_and_multiply(t, c):
            lo, hi = Z_CHUNKS[c]
            nc.scalar.activation(tanh[t][:, lo:hi], diff[t][:, lo:hi], ACT.Tanh)
            nc.vector.tensor_tensor(
                z[c][:, t, :], s_gained[t][:].indirect(list_cols(n2_sb, lo, hi)), tanh[t][:, lo:hi], ALU.mult
            )

        z_codes = tile("z_codes", [P, S], U32)
        z_scales = tile("z_scales", [P, S], U8)
        z_bf = [
            reuse.tile([P, HALF, PACK], BF16, name="z_bf%d" % c, offset=4 * TABLE + 2 * PACK * HALF * c, align_bytes=64)
            for c in range(2)
        ]

        scores_out(0)
        difference(0)
        for t in range(1, PACK):
            scores_out(t)
            difference(t)
            gained_out(t - 1)
            squash_and_multiply(t - 1, 0)
            if t == 1:
                squash_and_multiply(0, 1)
        gained_out(PACK - 1)
        squash_and_multiply(PACK - 1, 0)
        for t in range(1, PACK):
            squash_and_multiply(t, 1)
        interleave(nc.scalar.copy, z_bf[0][:], z[0][:])
        interleave(nc.vector.tensor_copy, z_bf[1][:, :Z_VECTOR_COLS, :], z[1][:, :, :Z_VECTOR_COLS])
        interleave(nc.scalar.copy, z_bf[1][:, Z_VECTOR_COLS:, :], z[1][:, :, Z_VECTOR_COLS:])
        for c, (lo, hi) in enumerate(Z_CHUNKS):
            nc.vector.quantize_mx(
                z_codes[:, lo:hi].bitcast(FP8X4), z_scales[:, lo:hi], z_bf[c][:].rearrange("p j t -> p (j t)")
            )

        w_dealt = [w_first]
        for t in range(1, PACK):
            w_later = reuse.tile(
                [P, P, 2], U8, name="w_later%d" % t, offset=4 * TABLE + 2 * PACK * HALF * min(t - 1, 1) + 2 * P * t, align_bytes=64
            )
            nc.vector.tensor_copy(w_later[:], w_columns[:, t, :, :])
            w_dealt.append(w_later)

        h_window = [tile("h_window%d" % t, [P, S], F32) for t in range(PACK)]
        for t in range(PACK):
            for c, (lo, hi) in enumerate(Z_CHUNKS):
                h_bank = psum.tile([P, hi - lo], F32, name="h_bank", tag="bank%d_%d" % (t, c))
                nc.tensor.matmul_mx(
                    h_bank[:],
                    lhsT=w_dealt[t][:].rearrange("p m e -> p (m e)").bitcast(FP4X4),
                    lhsT_scale=ws_dealt[:, P * t : P * (t + 1)],
                    rhs=z_codes[:, lo:hi].bitcast(FP8X4),
                    rhs_scale=z_scales[:, lo:hi],
                    start=True,
                    stop=True,
                )
                nc.scalar.copy(h_window[t][:, lo:hi], h_bank[:])

        out_codes = tile("out_codes", [P, S], U32)
        out_scales = tile("out_scales", [P, S], U8)
        out_rows = out_0.rearrange("(p t) j -> p t j", t=PACK)
        word_rows = out_1[0].rearrange("p j t -> p (j t)").bitcast(I32)
        fetched = [tile("fetched%d" % lo, [P, PACK, hi - lo], F32) for lo, hi in OUT_CHUNKS]
        result = [tile("result%d" % lo, [P, PACK, hi - lo], F32) for lo, hi in OUT_CHUNKS]
        result_bf = [tile("result_bf%d" % lo, [P, hi - lo, PACK], BF16) for lo, hi in OUT_CHUNKS]

        def fetch(c, t):
            lo, hi = OUT_CHUNKS[c]
            nc.vector.tensor_copy(fetched[c][:, t, :], h_window[t][:].indirect(list_cols(n3_sb, lo, hi)))

        def larger(c, t):
            lo, hi = OUT_CHUNKS[c]
            nc.vector.tensor_tensor(result[c][:, t, :], fetched[c][:, t, :], h_window[t][:, lo:hi], ALU.max)
            nc.sync.dma_start(out_rows[:, t, lo:hi], result[c][:, t, :])

        def planes(c):
            lo, hi = OUT_CHUNKS[c]
            for a in range(lo, hi, HALF):
                b = min(a + HALF, hi)
                nc.vector.quantize_mx(
                    out_codes[:, a:b].bitcast(FP8X4),
                    out_scales[:, a:b],
                    result_bf[c][:, a - lo : b - lo, :].rearrange("p j t -> p (j t)"),
                )
            nc.sync.dma_start(word_rows[:, lo:hi], out_codes[:].bitcast(I32)[:, lo:hi])

        steps = [(c, t) for c in range(len(OUT_CHUNKS)) for t in range(PACK)]
        last = len(OUT_CHUNKS) - 1
        fetch(*steps[0])
        for n, (c, t) in enumerate(steps):
            if n + 1 < len(steps):
                fetch(*steps[n + 1])
            larger(c, t)
            if c < last and t % 2 == 1:
                interleave(nc.scalar.copy, result_bf[c][:, :, t - 1 : t + 1], result[c][:, t - 1 : t + 1, :])
        planes(0)
        interleave(nc.vector.tensor_copy, result_bf[last][:], result[last][:])
        planes(last)
        scale_rows = out_2[0].bitcast(I32)
        for q in range(4):
            queue = nc.scalar if q % 2 == 0 else nc.sync
            queue.dma_start(scale_rows[4 * q : 4 * q + 4, :], out_scales[:].bitcast(I32)[32 * q : 32 * q + 4, :])
